import numpy as np
import ml_dtypes


def mxq(x, axis, fmt="e4m3"):
    dtype, down = {"e4m3": (ml_dtypes.float8_e4m3fn, 7), "e5m2": (ml_dtypes.float8_e5m2, 14)}[fmt]
    v = np.moveaxis(np.asarray(x, np.float32).astype(ml_dtypes.bfloat16).astype(np.float64), axis, -1)
    blocks = v.reshape(v.shape[:-1] + (-1, 32))
    amax = np.abs(blocks).max(-1, keepdims=True)
    byte = np.maximum(np.where(amax > 0, np.frexp(amax)[1] - 1 + 127, 0) - down, 1)
    scale = np.exp2(byte - 127.0)
    codes = (blocks / scale).astype(np.float32).astype(dtype).astype(np.float64)
    return np.moveaxis((codes * scale).reshape(v.shape), -1, axis)


WIDE = False


def mx_kscale(k):
    if not WIDE:
        return np.ones(k)
    levels = np.array([10, -10, 5, -5, 0])
    if k % 512:
        return np.exp2(np.random.permutation(np.resize(levels, k // 32))).repeat(32)
    a = np.empty((k // 512, 16))
    for p in range(k // 512):
        a[p, :8] = np.random.permutation(np.resize(levels, 8))
        for g in range(8):
            far = levels[np.abs(levels - a[p, g]) >= 10]
            a[p, g + 8] = far[np.random.randint(len(far))]
    return np.exp2(a.ravel()).repeat(32)


def f64(x):
    return np.asarray(x).astype(np.float64)


def striped(idx):
    return np.tile(idx.reshape(-1, 16).T, (8, 1)).astype(np.uint16)


def unstriped(offs):
    return offs[:16].T.reshape(-1).astype(np.int64)


E2M1 = np.array([0.0, 0.5, 1.0, 1.5, 2.0, 3.0, 4.0, 6.0, -0.0, -0.5, -1.0, -1.5, -2.0, -3.0, -4.0, -6.0])


def pack_weight(w, fmt):
    k, n = w.shape
    w = f64(np.asarray(w, np.float32).astype(ml_dtypes.bfloat16)).reshape(k // 32, 32, n)
    amax = np.abs(w).max(1)
    if fmt == "e4m3":
        byte = np.frexp(amax)[1] - 1 + 127 - 7
    else:
        mant, ex = np.frexp(amax / 6.0)
        byte = np.where(mant > 0.5, ex, ex - 1) + 127
    byte = np.clip(np.where(amax > 0, byte, 1), 1, 254)
    scaled = (w * np.exp2(127.0 - byte)[:, None, :]).reshape(k, n).astype(np.float32)
    by_word = np.ascontiguousarray(scaled.reshape(k // 512, 128, 4, n).transpose(0, 1, 3, 2))
    if fmt == "e4m3":
        words = by_word.astype(ml_dtypes.float8_e4m3fn).view(np.uint8)
    else:
        c = by_word.astype(ml_dtypes.float4_e2m1fn).view(np.uint8) & 0xF
        words = (c[..., 0::2] | (c[..., 1::2] << 4)).reshape(k // 512, 128, 2 * n)
    return np.ascontiguousarray(words), np.ascontiguousarray(byte.astype(np.uint8).reshape(k // 512, 16, n))


def unpack_weight(words, scales, fmt):
    g, _, n = scales.shape
    words = np.ascontiguousarray(words).reshape(g, 128, n, -1)
    if fmt == "e4m3":
        vals = words.view(ml_dtypes.float8_e4m3fn).astype(np.float64)
    else:
        nib = np.empty((g, 128, n, 4), np.uint8)
        nib[..., 0::2] = words & 0xF
        nib[..., 1::2] = words >> 4
        vals = E2M1[nib]
    vals = vals * np.repeat(np.exp2(scales.astype(np.float64) - 127.0), 8, axis=1)[..., None]
    return vals.transpose(0, 1, 3, 2).reshape(g * 512, n)


def pack_table(v):
    words, scales = pack_weight(v, "e4m3")
    return np.concatenate([words.reshape(words.shape[0], -1), scales.reshape(scales.shape[0], -1)], axis=1)


def unpack_table(tab):
    g, t = tab.shape[0], tab.shape[1] // 528
    return unpack_weight(tab[:, :512 * t].reshape(g, 128, t, 4), tab[:, 512 * t:].reshape(g, 16, t), "e4m3")


def silu(v):
    return v / (1.0 + np.exp(-np.maximum(v, -700.0)))


K, M, T, S = 1024, 128, 4096, 512


def setup_inputs():
    n = np.random.standard_normal
    s = mx_kscale(K)[:, None]
    p_w0 = pack_weight(n((K, M)) / np.sqrt(3 * K) / s, "e2m1")
    p_w1 = pack_weight(n((K, M)) / np.sqrt(3 * K) / s, "e4m3")
    return {
        "tab": pack_table(n((K, T)) * s),
        "w0_words": p_w0[0],
        "w0_scales": p_w0[1],
        "w1_words": p_w1[0],
        "w1_scales": p_w1[1],
        "w2": (n((K, M)) / np.sqrt(3 * K) / s).astype(np.float32),
        "b": (0.3 * n(128)).astype(np.float32),
        "offs": striped(np.concatenate([np.random.permutation(T)[:S] for _ in range(3)])),
    }


def reference(tab, w0_words, w0_scales, w1_words, w1_scales, w2, b, offs):
    v = unpack_table(tab)
    idx = unstriped(offs).reshape(3, S)
    w0_ = unpack_weight(w0_words, w0_scales, "e2m1")
    w1_ = unpack_weight(w1_words, w1_scales, "e4m3")
    w2_ = mxq(f64(w2), 0, "e4m3")
    y = v[:, idx[0]].T @ w0_ + v[:, idx[1]].T @ w1_ + v[:, idx[2]].T @ w2_
    return silu(y + f64(b)[None, :])

@@ -1,0 +1,158 @@
+from contextlib import ExitStack
+
+import concourse.mybir as mybir
+from concourse.masks import make_identity
+
+K, M, T, S = 1024, 128, 4096, 512
+FIELDS = 3
+FLOPS = 2 * FIELDS * K * M * S
+
+F32 = mybir.dt.float32
+BF16 = mybir.dt.bfloat16
+I32 = mybir.dt.int32
+U32 = mybir.dt.uint32
+U16 = mybir.dt.uint16
+U8 = mybir.dt.uint8
+FP8X4 = mybir.dt.float8_e4m3fn_x4
+FP4X4 = mybir.dt.float4_e2m1fn_x4
+ACT = mybir.ActivationFunctionType
+ALU = mybir.AluOpType
+
+P = 128
+PACK = 4
+PASSES = K // (P * PACK)
+BLOCKS = 16
+ROWS = 4
+QUAD = 32
+CHUNKS = S // P
+LIST_COLS = S // 16
+
+
+def tile_list_tabfield_tm_silu_kernel(
+    tc, tab, w0_words, w0_scales, w1_words, w1_scales, w2, b, offs, out
+):
+    nc = tc.nc
+    with ExitStack() as ctx:
+        keep = ctx.enter_context(tc.tile_pool(name="keep", bufs=1))
+        psum = ctx.enter_context(tc.psum_pool(name="psum", bufs=1))
+
+        offsets = keep.tile([P, FIELDS * LIST_COLS], U16, name="offsets")
+        nc.sync.dma_start(offsets[:], offs)
+
+        def table_words(a):
+            return tab[a, 0 : P * PACK * T].bitcast(I32).rearrange("(p t) -> p t", p=P)
+
+        words = [keep.tile([P, T], U32, name=f"words{a}", align_bytes=64) for a in range(PASSES)]
+        w0w = keep.tile([P, PASSES, 2 * M], U8, name="w0w", align_bytes=64)
+        w1w = keep.tile([P, PASSES, M], U32, name="w1w", align_bytes=64)
+        nc.sync.dma_start(words[0][:].bitcast(I32), table_words(0))
+        nc.sync.dma_start(w0w[:].bitcast(I32), w0_words.bitcast(I32).rearrange("a p n -> p a n"))
+        nc.sync.dma_start(
+            w1w[:].bitcast(I32),
+            w1_words.rearrange("a p n t -> a p (n t)").bitcast(I32).rearrange("a p n -> p a n"),
+        )
+        nc.sync.dma_start(words[1][:].bitcast(I32), table_words(1))
+
+        scale_window = keep.tile([P, T], U8, name="scale_window", tag="early_late", align_bytes=64)
+        nc.vector.memset(scale_window[:].bitcast(I32), 0)
+        for a in range(PASSES):
+            rows = tab[a, P * PACK * T :].bitcast(I32).rearrange("(q t) -> q t", q=BLOCKS)
+            nc.scalar.dma_start(scale_window[ROWS * a : P : 8, :].bitcast(I32), rows)
+
+        planes = keep.tile([P, PASSES, FIELDS * S], U8, name="planes", align_bytes=64)
+        nc.vector.memset(planes[:].bitcast(I32), 0)
+
+        b_col = keep.tile([P, 1], F32, name="b_col")
+        nc.gpsimd.dma_start(b_col[:], b.rearrange("(p o) -> p o", o=1))
+        w0s = keep.tile([P, PASSES, M], U8, name="w0s", align_bytes=64)
+        w1s = keep.tile([P, PASSES, M], U8, name="w1s", align_bytes=64)
+        nc.gpsimd.memset(w0s[:].bitcast(I32), 0)
+        nc.gpsimd.memset(w1s[:].bitcast(I32), 0)
+        ident = keep.tile([P, P], F32, name="ident")
+        make_identity(nc, ident[:])
+        for plane, scales in ((w0s, w0_scales), (w1s, w1_scales)):
+            by_row = scales.bitcast(I32).rearrange("a (Q r) n -> r Q a n", r=ROWS)
+            for r in range(ROWS):
+                nc.gpsimd.dma_start(plane[r:P:QUAD, :, :].bitcast(I32), by_row[r])
+
+        b_psum = psum.tile([P, M], F32, name="b_psum")
+        nc.tensor.transpose(b_psum[:], b_col[:].to_broadcast([P, P]), ident[:])
+        bias = keep.tile([P, M], F32, name="bias")
+        nc.scalar.copy(bias[:], b_psum[:])
+        warm = keep.tile([P, 1], F32, name="warm")
+        nc.scalar.activation(warm[:], bias[:, 0:1], ACT.Silu)
+
+        picked_scales = keep.tile([P, FIELDS * S], U8, name="picked_scales", align_bytes=64)
+        nc.vector.tensor_copy(picked_scales[:], scale_window[:].indirect(offsets[:]))
+
+        def move_scales(a):
+            for r in range(ROWS):
+                nc.sync.dma_start(
+                    planes[r:P:QUAD, a, :].bitcast(I32),
+                    picked_scales[8 * r + ROWS * a : P : QUAD, :].bitcast(I32),
+                )
+
+        move_scales(0)
+        w2_raw = keep.tile([P, PASSES, PACK, M], F32, name="w2_raw", tag="early_late", align_bytes=64)
+        nc.sync.dma_start(w2_raw[:], w2.rearrange("(a p j) n -> p a j n", p=P, j=PACK))
+        move_scales(1)
+
+        picked0 = keep.tile([P, FIELDS * S], U32, name="picked0", align_bytes=64)
+        nc.vector.tensor_copy(picked0[:], words[0][:].indirect(offsets[:]))
+        picked = {(0, f): picked0[:, f * S : (f + 1) * S] for f in range(FIELDS)}
+
+        def gather_pass1(f, tag):
+            dst = keep.tile([P, S], U32, name=f"picked1_{f}", tag=tag, align_bytes=64)
+            nc.vector.tensor_copy(
+                dst[:], words[1][:].indirect(offsets[:, f * LIST_COLS : (f + 1) * LIST_COLS])
+            )
+            picked[(1, f)] = dst[:]
+
+        gather_pass1(0, "picked1_0")
+        gather_pass1(1, "picked1_1")
+
+        w2w = [keep.tile([P, M], U32, name=f"w2w{a}", align_bytes=64) for a in range(PASSES)]
+        w2s = [keep.tile([P, M], U8, name=f"w2s{a}", align_bytes=64) for a in range(PASSES)]
+
+        def quantise_w2(a, tag):
+            grouped = keep.tile([P, M, PACK], BF16, name=f"w2_grouped{a}", tag=tag, align_bytes=64)
+            nc.scalar.copy(grouped[:], w2_raw[:, a, :, :].rearrange("p j n -> p n j"))
+            nc.vector.quantize_mx(
+                out=w2w[a][:].bitcast(FP8X4),
+                scales=w2s[a][:],
+                in_=grouped[:].rearrange("p n j -> p (n j)"),
+            )
+
+        quantise_w2(0, "last_gather")
+        gather_pass1(2, "last_gather")
+        quantise_w2(1, "w2_grouped1")
+
+        def weight(f, a):
+            if f == 0:
+                return w0w[:, a, :].bitcast(FP4X4), w0s[:, a, :]
+            if f == 1:
+                return w1w[:, a, :].bitcast(FP8X4), w1s[:, a, :]
+            return w2w[a][:].bitcast(FP8X4), w2s[a][:]
+
+        acc = [psum.tile([P, M], F32, name=f"acc{c}") for c in range(CHUNKS)]
+        order = [(0, 0), (1, 0), (0, 1), (1, 1), (2, 0), (2, 1)]
+        for step, (f, a) in enumerate(order):
+            codes, scales = weight(f, a)
+            for c in range(CHUNKS):
+                nc.tensor.matmul_mx(
+                    out=acc[c][:],
+                    lhsT=picked[(a, f)][:, c * P : (c + 1) * P].bitcast(FP8X4),
+                    lhsT_scale=planes[:, a, f * S + c * P : f * S + (c + 1) * P],
+                    rhs=codes,
+                    rhs_scale=scales,
+                    start=(step == 0),
+                    stop=(step == len(order) - 1),
+                )
+
+        for c in range(CHUNKS):
+            summed = keep.tile([P, M], F32, name=f"summed{c}")
+            nc.vector.tensor_tensor(summed[:], acc[c][:], bias[:], ALU.add)
+            result = keep.tile([P, M], F32, name=f"result{c}")
+            nc.scalar.activation(result[:], summed[:], ACT.Silu)
+            queue = nc.scalar if c == CHUNKS - 1 else nc.sync
+            queue.dma_start(out[c * P : (c + 1) * P, :], result[:])

@@ -45,35 +45,42 @@ def tile_list_tabfield_tm_silu_kernel(
         words = [keep.tile([P, T], U32, name=f"words{a}", align_bytes=64) for a in range(PASSES)]
         w0w = keep.tile([P, PASSES, 2 * M], U8, name="w0w", align_bytes=64)
         w1w = keep.tile([P, PASSES, M], U32, name="w1w", align_bytes=64)
-        nc.sync.dma_start(words[0][:].bitcast(I32), table_words(0))
-        nc.sync.dma_start(w0w[:].bitcast(I32), w0_words.bitcast(I32).rearrange("a p n -> p a n"))
-        nc.sync.dma_start(
-            w1w[:].bitcast(I32),
-            w1_words.rearrange("a p n t -> a p (n t)").bitcast(I32).rearrange("a p n -> p a n"),
-        )
-        nc.sync.dma_start(words[1][:].bitcast(I32), table_words(1))
-
+        HEAD = 1024
+        nc.sync.dma_start(words[0][:, 0:HEAD].bitcast(I32), table_words(0)[:, 0:HEAD])
         scale_window = keep.tile([P, T], U8, name="scale_window", tag="early_late", align_bytes=64)
         nc.vector.memset(scale_window[:].bitcast(I32), 0)
         for a in range(PASSES):
             rows = tab[a, P * PACK * T :].bitcast(I32).rearrange("(q t) -> q t", q=BLOCKS)
-            nc.scalar.dma_start(scale_window[ROWS * a : P : 8, :].bitcast(I32), rows)
+            nc.sync.dma_start(scale_window[ROWS * a : P : 8, :].bitcast(I32), rows)
+        nc.sync.dma_start(words[0][:, HEAD:T].bitcast(I32), table_words(0)[:, HEAD:T])
+        w0s = keep.tile([P, PASSES, M], U8, name="w0s", align_bytes=64)
+        w1s = keep.tile([P, PASSES, M], U8, name="w1s", align_bytes=64)
+
+        def load_weight_scales(plane, scales):
+            by_row = scales.bitcast(I32).rearrange("a (Q r) n -> r Q a n", r=ROWS)
+            for r in range(ROWS):
+                nc.sync.dma_start(plane[r:P:QUAD, :, :].bitcast(I32), by_row[r])
+
+        nc.gpsimd.memset(w0s[:].bitcast(I32), 0)
+        nc.gpsimd.memset(w1s[:].bitcast(I32), 0)
+        nc.sync.dma_start(w0w[:].bitcast(I32), w0_words.bitcast(I32).rearrange("a p n -> p a n"))
+        load_weight_scales(w0s, w0_scales)
+        nc.sync.dma_start(
+            w1w[:].bitcast(I32),
+            w1_words.rearrange("a p n t -> a p (n t)").bitcast(I32).rearrange("a p n -> p a n"),
+        )
+        HALF = T // 2
+        nc.sync.dma_start(words[1][:, 0:HALF].bitcast(I32), table_words(1)[:, 0:HALF])
+        load_weight_scales(w1s, w1_scales)
+        nc.sync.dma_start(words[1][:, HALF:T].bitcast(I32), table_words(1)[:, HALF:T])
 
         planes = keep.tile([P, PASSES, FIELDS * S], U8, name="planes", align_bytes=64)
         nc.vector.memset(planes[:].bitcast(I32), 0)
 
         b_col = keep.tile([P, 1], F32, name="b_col")
         nc.gpsimd.dma_start(b_col[:], b.rearrange("(p o) -> p o", o=1))
-        w0s = keep.tile([P, PASSES, M], U8, name="w0s", align_bytes=64)
-        w1s = keep.tile([P, PASSES, M], U8, name="w1s", align_bytes=64)
-        nc.gpsimd.memset(w0s[:].bitcast(I32), 0)
-        nc.gpsimd.memset(w1s[:].bitcast(I32), 0)
         ident = keep.tile([P, P], F32, name="ident")
         make_identity(nc, ident[:])
-        for plane, scales in ((w0s, w0_scales), (w1s, w1_scales)):
-            by_row = scales.bitcast(I32).rearrange("a (Q r) n -> r Q a n", r=ROWS)
-            for r in range(ROWS):
-                nc.gpsimd.dma_start(plane[r:P:QUAD, :, :].bitcast(I32), by_row[r])
 
         b_psum = psum.tile([P, M], F32, name="b_psum")
         nc.tensor.transpose(b_psum[:], b_col[:].to_broadcast([P, P]), ident[:])
@@ -92,9 +99,13 @@ def tile_list_tabfield_tm_silu_kernel(
                     picked_scales[8 * r + ROWS * a : P : QUAD, :].bitcast(I32),
                 )
 
+        w2_raw = keep.tile([P, PACK, M], F32, name="w2_raw", align_bytes=64)
+        w2_late = keep.tile([P, PACK, M], F32, name="w2_late", tag="early_late", align_bytes=64)
+        w2_rows = w2.rearrange("(a p j) n -> a p j n", p=P, j=PACK)
+        nc.sync.dma_start(w2_raw[:], w2_rows[0])
         move_scales(0)
-        w2_raw = keep.tile([P, PASSES, PACK, M], F32, name="w2_raw", tag="early_late", align_bytes=64)
-        nc.sync.dma_start(w2_raw[:], w2.rearrange("(a p j) n -> p a j n", p=P, j=PACK))
+        nc.sync.dma_start(w2_late[:], w2_rows[1])
+        w2_f32 = [w2_raw, w2_late]
         move_scales(1)
 
         picked0 = keep.tile([P, FIELDS * S], U32, name="picked0", align_bytes=64)
@@ -116,7 +127,7 @@ def tile_list_tabfield_tm_silu_kernel(
 
         def quantise_w2(a, tag):
             grouped = keep.tile([P, M, PACK], BF16, name=f"w2_grouped{a}", tag=tag, align_bytes=64)
-            nc.scalar.copy(grouped[:], w2_raw[:, a, :, :].rearrange("p j n -> p n j"))
+            nc.scalar.copy(grouped[:], w2_f32[a][:].rearrange("p j n -> p n j"))
             nc.vector.quantize_mx(
                 out=w2w[a][:].bitcast(FP8X4),
                 scales=w2s[a][:],

from contextlib import ExitStack

import concourse.mybir as mybir
from concourse.masks import make_identity

K, M, T, S = 1024, 128, 4096, 512
FIELDS = 3
FLOPS = 2 * FIELDS * K * M * S

F32 = mybir.dt.float32
BF16 = mybir.dt.bfloat16
I32 = mybir.dt.int32
U32 = mybir.dt.uint32
U16 = mybir.dt.uint16
U8 = mybir.dt.uint8
FP8X4 = mybir.dt.float8_e4m3fn_x4
FP4X4 = mybir.dt.float4_e2m1fn_x4
ACT = mybir.ActivationFunctionType
ALU = mybir.AluOpType

P = 128
PACK = 4
PASSES = K // (P * PACK)
BLOCKS = 16
ROWS = 4
QUAD = 32
CHUNKS = S // P
LIST_COLS = S // 16


def tile_list_tabfield_tm_silu_kernel(
    tc, tab, w0_words, w0_scales, w1_words, w1_scales, w2, b, offs, out
):
    nc = tc.nc
    with ExitStack() as ctx:
        keep = ctx.enter_context(tc.tile_pool(name="keep", bufs=1))
        psum = ctx.enter_context(tc.psum_pool(name="psum", bufs=1))

        offsets = keep.tile([P, FIELDS * LIST_COLS], U16, name="offsets")
        nc.sync.dma_start(offsets[:], offs)

        def table_words(a):
            return tab[a, 0 : P * PACK * T].bitcast(I32).rearrange("(p t) -> p t", p=P)

        words = [keep.tile([P, T], U32, name=f"words{a}", align_bytes=64) for a in range(PASSES)]
        w0w = keep.tile([P, PASSES, 2 * M], U8, name="w0w", align_bytes=64)
        w1w = keep.tile([P, PASSES, M], U32, name="w1w", align_bytes=64)
        HEAD = 1024
        nc.sync.dma_start(words[0][:, 0:HEAD].bitcast(I32), table_words(0)[:, 0:HEAD])
        scale_window = keep.tile([P, T], U8, name="scale_window", tag="early_late", align_bytes=64)
        nc.vector.memset(scale_window[:].bitcast(I32), 0)
        for a in range(PASSES):
            rows = tab[a, P * PACK * T :].bitcast(I32).rearrange("(q t) -> q t", q=BLOCKS)
            nc.sync.dma_start(scale_window[ROWS * a : P : 8, :].bitcast(I32), rows)
        nc.sync.dma_start(words[0][:, HEAD:T].bitcast(I32), table_words(0)[:, HEAD:T])
        w0s = keep.tile([P, PASSES, M], U8, name="w0s", align_bytes=64)
        w1s = keep.tile([P, PASSES, M], U8, name="w1s", align_bytes=64)

        def load_weight_scales(plane, scales):
            by_row = scales.bitcast(I32).rearrange("a (Q r) n -> r Q a n", r=ROWS)
            for r in range(ROWS):
                nc.sync.dma_start(plane[r:P:QUAD, :, :].bitcast(I32), by_row[r])

        nc.gpsimd.memset(w0s[:].bitcast(I32), 0)
        nc.gpsimd.memset(w1s[:].bitcast(I32), 0)
        nc.sync.dma_start(w0w[:].bitcast(I32), w0_words.bitcast(I32).rearrange("a p n -> p a n"))
        load_weight_scales(w0s, w0_scales)
        nc.sync.dma_start(
            w1w[:].bitcast(I32),
            w1_words.rearrange("a p n t -> a p (n t)").bitcast(I32).rearrange("a p n -> p a n"),
        )
        HALF = T // 2
        nc.sync.dma_start(words[1][:, 0:HALF].bitcast(I32), table_words(1)[:, 0:HALF])
        load_weight_scales(w1s, w1_scales)
        nc.sync.dma_start(words[1][:, HALF:T].bitcast(I32), table_words(1)[:, HALF:T])

        planes = keep.tile([P, PASSES, FIELDS * S], U8, name="planes", align_bytes=64)
        nc.vector.memset(planes[:].bitcast(I32), 0)

        b_col = keep.tile([P, 1], F32, name="b_col")
        nc.gpsimd.dma_start(b_col[:], b.rearrange("(p o) -> p o", o=1))
        ident = keep.tile([P, P], F32, name="ident")
        make_identity(nc, ident[:])

        b_psum = psum.tile([P, M], F32, name="b_psum")
        nc.tensor.transpose(b_psum[:], b_col[:].to_broadcast([P, P]), ident[:])
        bias = keep.tile([P, M], F32, name="bias")
        nc.scalar.copy(bias[:], b_psum[:])
        warm = keep.tile([P, 1], F32, name="warm")
        nc.scalar.activation(warm[:], bias[:, 0:1], ACT.Silu)

        picked_scales = keep.tile([P, FIELDS * S], U8, name="picked_scales", align_bytes=64)
        nc.vector.tensor_copy(picked_scales[:], scale_window[:].indirect(offsets[:]))

        def move_scales(a):
            for r in range(ROWS):
                nc.sync.dma_start(
                    planes[r:P:QUAD, a, :].bitcast(I32),
                    picked_scales[8 * r + ROWS * a : P : QUAD, :].bitcast(I32),
                )

        w2_raw = keep.tile([P, PACK, M], F32, name="w2_raw", align_bytes=64)
        w2_late = keep.tile([P, PACK, M], F32, name="w2_late", tag="early_late", align_bytes=64)
        w2_rows = w2.rearrange("(a p j) n -> a p j n", p=P, j=PACK)
        nc.sync.dma_start(w2_raw[:], w2_rows[0])
        move_scales(0)
        nc.sync.dma_start(w2_late[:], w2_rows[1])
        w2_f32 = [w2_raw, w2_late]
        move_scales(1)

        picked0 = keep.tile([P, FIELDS * S], U32, name="picked0", align_bytes=64)
        nc.vector.tensor_copy(picked0[:], words[0][:].indirect(offsets[:]))
        picked = {(0, f): picked0[:, f * S : (f + 1) * S] for f in range(FIELDS)}

        def gather_pass1(f, tag):
            dst = keep.tile([P, S], U32, name=f"picked1_{f}", tag=tag, align_bytes=64)
            nc.vector.tensor_copy(
                dst[:], words[1][:].indirect(offsets[:, f * LIST_COLS : (f + 1) * LIST_COLS])
            )
            picked[(1, f)] = dst[:]

        gather_pass1(0, "picked1_0")
        gather_pass1(1, "picked1_1")

        w2w = [keep.tile([P, M], U32, name=f"w2w{a}", align_bytes=64) for a in range(PASSES)]
        w2s = [keep.tile([P, M], U8, name=f"w2s{a}", align_bytes=64) for a in range(PASSES)]

        def quantise_w2(a, tag):
            grouped = keep.tile([P, M, PACK], BF16, name=f"w2_grouped{a}", tag=tag, align_bytes=64)
            nc.scalar.copy(grouped[:], w2_f32[a][:].rearrange("p j n -> p n j"))
            nc.vector.quantize_mx(
                out=w2w[a][:].bitcast(FP8X4),
                scales=w2s[a][:],
                in_=grouped[:].rearrange("p n j -> p (n j)"),
            )

        quantise_w2(0, "last_gather")
        gather_pass1(2, "last_gather")
        quantise_w2(1, "w2_grouped1")

        def weight(f, a):
            if f == 0:
                return w0w[:, a, :].bitcast(FP4X4), w0s[:, a, :]
            if f == 1:
                return w1w[:, a, :].bitcast(FP8X4), w1s[:, a, :]
            return w2w[a][:].bitcast(FP8X4), w2s[a][:]

        acc = [psum.tile([P, M], F32, name=f"acc{c}") for c in range(CHUNKS)]
        order = [(0, 0), (1, 0), (0, 1), (1, 1), (2, 0), (2, 1)]
        for step, (f, a) in enumerate(order):
            codes, scales = weight(f, a)
            for c in range(CHUNKS):
                nc.tensor.matmul_mx(
                    out=acc[c][:],
                    lhsT=picked[(a, f)][:, c * P : (c + 1) * P].bitcast(FP8X4),
                    lhsT_scale=planes[:, a, f * S + c * P : f * S + (c + 1) * P],
                    rhs=codes,
                    rhs_scale=scales,
                    start=(step == 0),
                    stop=(step == len(order) - 1),
                )

        for c in range(CHUNKS):
            summed = keep.tile([P, M], F32, name=f"summed{c}")
            nc.vector.tensor_tensor(summed[:], acc[c][:], bias[:], ALU.add)
            result = keep.tile([P, M], F32, name=f"result{c}")
            nc.scalar.activation(result[:], summed[:], ACT.Silu)
            queue = nc.scalar if c == CHUNKS - 1 else nc.sync
            queue.dma_start(out[c * P : (c + 1) * P, :], result[:])
